import numpy as np
import ml_dtypes


def mxq(x, axis, fmt="e4m3"):
    dtype, down = {"e4m3": (ml_dtypes.float8_e4m3fn, 7), "e5m2": (ml_dtypes.float8_e5m2, 14)}[fmt]
    v = np.moveaxis(np.asarray(x, np.float32).astype(ml_dtypes.bfloat16).astype(np.float64), axis, -1)
    blocks = v.reshape(v.shape[:-1] + (-1, 32))
    amax = np.abs(blocks).max(-1, keepdims=True)
    byte = np.maximum(np.where(amax > 0, np.frexp(amax)[1] - 1 + 127, 0) - down, 1)
    scale = np.exp2(byte - 127.0)
    codes = (blocks / scale).astype(np.float32).astype(dtype).astype(np.float64)
    return np.moveaxis((codes * scale).reshape(v.shape), -1, axis)


WIDE = False


def mx_kscale(k):
    if not WIDE:
        return np.ones(k)
    levels = np.array([10, -10, 5, -5, 0])
    if k % 512:
        return np.exp2(np.random.permutation(np.resize(levels, k // 32))).repeat(32)
    a = np.empty((k // 512, 16))
    for p in range(k // 512):
        a[p, :8] = np.random.permutation(np.resize(levels, 8))
        for g in range(8):
            far = levels[np.abs(levels - a[p, g]) >= 10]
            a[p, g + 8] = far[np.random.randint(len(far))]
    return np.exp2(a.ravel()).repeat(32)


def f64(x):
    return np.asarray(x).astype(np.float64)


def striped(idx):
    return np.tile(idx.reshape(-1, 16).T, (8, 1)).astype(np.uint16)


def unstriped(offs):
    return offs[:16].T.reshape(-1).astype(np.int64)


def striped8(idx):
    return np.concatenate([x.reshape(-1, 16).T for x in idx]).astype(np.uint16)


def runs(offs, k):
    lists = np.stack([offs[16 * r : 16 * r + 16].T.reshape(-1) for r in range(8)]).astype(np.int64)
    return lists[np.arange(k) % 512 // 64]


def pack_weight(w):
    k, n = w.shape
    w = f64(np.asarray(w, np.float32).astype(ml_dtypes.bfloat16)).reshape(k // 32, 32, n)
    amax = np.abs(w).max(1)
    byte = np.clip(np.where(amax > 0, np.frexp(amax)[1] - 1 + 127 - 7, 1), 1, 254)
    scaled = (w * np.exp2(127.0 - byte)[:, None, :]).reshape(k, n).astype(np.float32)
    words = np.ascontiguousarray(scaled.reshape(k // 512, 128, 4, n).transpose(0, 1, 3, 2)).astype(ml_dtypes.float8_e4m3fn).view(np.uint8)
    return words, np.ascontiguousarray(byte.astype(np.uint8).reshape(k // 512, 16, n))


def unpack_weight(words, scales):
    g, p, n, _ = words.shape
    vals = np.ascontiguousarray(words).view(ml_dtypes.float8_e4m3fn).astype(np.float64) * np.repeat(np.exp2(scales.astype(np.float64) - 127.0), 8, axis=1)[..., None]
    return vals.transpose(0, 1, 3, 2).reshape(g * 512, n)


def sigmoid(v):
    return 1.0 / (1.0 + np.exp(-np.maximum(v, -700.0)))


K, T, S, N, G, H = 512, 2048, 512, 512, 2048, 512


def setup_inputs():
    n = np.random.standard_normal
    s = mx_kscale(K)[:, None]
    u = mx_kscale(S)
    packed_xT = pack_weight(n((K, T)) * s)
    packed_dT = pack_weight(n((K, G)) / s)
    return {
        "x_words": packed_xT[0],
        "x_scales": packed_xT[1],
        "d_words": packed_dT[0],
        "d_scales": packed_dT[1],
        "tau": np.random.uniform(0.3, 0.9, (H, 1)).astype(np.float32),
        "gn": (np.random.uniform(0.5, 1.5, (H, 1)) * u[:, None]).astype(np.float32),
        "w1": (n((H, N)) / np.sqrt(2 * H) / u[:, None]).astype(np.float32),
        "w2": (n((K, N)) / np.sqrt(2 * K) / s).astype(np.float32),
        "sl": np.random.uniform(1.0, 2.0, (N, 1)).astype(np.float32),
        "th": (0.5 * n((N, 1))).astype(np.float32),
        "offs": striped(np.random.permutation(T)[:S]),
        "k1": striped8(np.random.randint(0, G, (8, H))),
        "n1": striped8(np.stack([np.random.permutation(S) for _ in range(8)])),
        "n2": striped8(np.stack([np.random.permutation(S) for _ in range(8)])),
        "two": striped(np.random.permutation(T)[:S]),
        "n3": striped8(np.stack([np.random.permutation(S) for _ in range(8)])),
    }


def reference(x_words, x_scales, d_words, d_scales, tau, gn, w1, w2, sl, th, offs, k1, n1, n2, two, n3):
    d_k1 = unpack_weight(d_words, d_scales)[np.arange(K)[:, None], runs(k1, K)]
    xq = unpack_weight(x_words, x_scales)[:, unstriped(offs)]
    s = 0.0625 * (d_k1.T @ xq)
    top = s.max(axis=1, keepdims=True)
    ea = np.exp(f64(tau) * (s[np.arange(H)[:, None], runs(n2, H)] - top))
    z = f64(gn) * ((0.5 * (s - (s[np.arange(H)[:, None], runs(n1, H)]))) / (ea + 0.25))
    x_two = unpack_weight(x_words, x_scales)[:, unstriped(two)]
    h = mxq(f64(w1), 0, "e4m3").T @ mxq(z, 0, "e4m3") + mxq(f64(w2), 0, "e4m3").T @ x_two
    sg = sigmoid(f64(sl) * (h[np.arange(N)[:, None], runs(n3, N)] - f64(th)))
    return h * sg

@@ -1,0 +1,223 @@
+from contextlib import ExitStack
+
+import concourse.mybir as mybir
+
+K, T, S, N, G, H = 512, 2048, 512, 512, 2048, 512
+FLOPS = 3 * 2 * 512 * 512 * 512
+
+F32 = mybir.dt.float32
+BF16 = mybir.dt.bfloat16
+I32 = mybir.dt.int32
+U32 = mybir.dt.uint32
+U16 = mybir.dt.uint16
+U8 = mybir.dt.uint8
+FP8X4 = mybir.dt.float8_e4m3fn_x4
+ALU = mybir.AluOpType
+ACT = mybir.ActivationFunctionType
+
+P = 128
+PACK = 4
+HALF = S // 2
+CHUNK = 128
+ACT_GATHERS = (1, 2, 3)
+
+
+def tile_picked_kmixeraesa_none_p_kernel(
+    tc, x_words, x_scales, d_words, d_scales, tau, gn, w1, w2, sl, th, offs, k1, n1, n2, two, n3, out
+):
+    nc = tc.nc
+    with ExitStack() as ctx:
+        keep = ctx.enter_context(tc.tile_pool(name="keep", bufs=1))
+        psum = ctx.enter_context(tc.psum_pool(name="psum", bufs=1))
+
+        def load_list(name, src):
+            tile = keep.tile([P, S // 16], U16, name=name)
+            nc.sync.dma_start(tile[:], src)
+            return tile
+
+        def load_words(name, src):
+            tile = keep.tile([P, T], U32, name=name, align_bytes=64)
+            nc.sync.dma_start(tile[:].bitcast(I32), src[0].rearrange("p n t -> p (n t)").bitcast(I32))
+            return tile
+
+
+        def load_weight(name, src, tag):
+            tile = keep.tile([P, PACK, N], F32, name=name, tag=tag, align_bytes=64)
+            nc.sync.dma_start(tile[:], src.rearrange("(p j) n -> p j n", j=PACK))
+            return tile
+
+        def halves(lst):
+            return [lst[:, 16 * a : 16 * (a + 1)] for a in range(2)]
+
+        d_bytes = keep.tile([P, G], U8, name="d_bytes", align_bytes=64)
+        x_bytes = keep.tile([P, T], U8, name="x_bytes", align_bytes=64)
+        key_plane = keep.tile([P, H], U8, name="key_plane", align_bytes=64)
+        nc.gpsimd.memset(d_bytes[:].bitcast(I32), 0)
+        nc.vector.memset(x_bytes[:].bitcast(I32), 0)
+        nc.vector.memset(key_plane[:].bitcast(I32), 0)
+
+        nc.gpsimd.dma_start(d_bytes[0:P:8, :].bitcast(I32), d_scales[0].bitcast(I32))
+        k1_t = load_list("k1_t", k1)
+        offs_t = load_list("offs_t", offs)
+        for q in range(4):
+            nc.scalar.dma_start(x_bytes[32 * q : 32 * q + 4, :].bitcast(I32), x_scales[0, 4 * q : 4 * q + 4, :].bitcast(I32))
+        two_t = load_list("two_t", two)
+        n2_t = load_list("n2_t", n2)
+        d_table = load_words("d_table", d_words)
+        n1_t = load_list("n1_t", n1)
+        n3_t = load_list("n3_t", n3)
+        x_table = load_words("x_table", x_words)
+
+        key_bytes = keep.tile([P, H], U8, name="key_bytes", tag="stage0", align_bytes=64)
+        nc.vector.tensor_copy(key_bytes[:], d_bytes[:].indirect(k1_t[:]))
+        key_bytes_dealt = keep.tile([P, H], U8, name="key_bytes_dealt", tag="stage1", align_bytes=64)
+        nc.vector.tensor_copy(
+            key_bytes_dealt[:].rearrange("p (t m) -> p m t", t=PACK), key_bytes[:].rearrange("p (m t) -> p m t", t=PACK)
+        )
+        for r in range(4):
+            queue = nc.gpsimd if r == 0 else nc.scalar
+            queue.dma_start(key_plane[r:P:32, :].bitcast(I32), key_bytes_dealt[8 * r : P : 32, :].bitcast(I32))
+        columns = keep.tile([P, 32], F32, name="columns", tag="stage0", align_bytes=64)
+        tau_t, gn_t, sl_t, th_t = [columns[:, 8 * u : 8 * u + PACK] for u in range(4)]
+        for dst, src in ((tau_t, tau), (gn_t, gn), (sl_t, sl), (th_t, th)):
+            nc.gpsimd.dma_start(dst, src.rearrange("(p t) o -> p (t o)", t=PACK))
+        key_words = keep.tile([P, H], U32, name="key_words", tag="stage2", align_bytes=64)
+        nc.vector.tensor_copy(key_words[:], d_table[:].indirect(k1_t[:]))
+        key_codes = keep.tile([P, H], U32, name="key_codes", align_bytes=64)
+        nc.vector.tensor_copy(
+            key_codes[:].bitcast(I32).rearrange("p (t m) -> p m t", t=PACK),
+            key_words[:].bitcast(I32).rearrange("p (m t) -> p m t", t=PACK),
+        )
+        w1_raw = load_weight("w1_raw", w1, "stage2")
+        w2_raw = load_weight("w2_raw", w2, "stage1")
+        tok_plane = keep.tile([P, S], U8, name="tok_plane", align_bytes=64)
+        nc.vector.tensor_copy(tok_plane[:], x_bytes[:].indirect(offs_t[:]))
+        tok_codes = []
+        for a, part in enumerate(halves(offs_t)):
+            codes = keep.tile([P, HALF], U32, name=f"tok_codes{a}", align_bytes=64)
+            nc.vector.tensor_copy(codes[:], x_table[:].indirect(part))
+            tok_codes.append(codes)
+
+        s_bank = [psum.tile([P, S], F32, name=f"s_bank{t}") for t in range(PACK)]
+        for a in range(2):
+            for t in range(PACK):
+                nc.tensor.matmul_mx(
+                    s_bank[t][:, a * HALF : (a + 1) * HALF],
+                    lhsT=key_codes[:, t * P : (t + 1) * P].bitcast(FP8X4),
+                    lhsT_scale=key_plane[:, t * P : (t + 1) * P],
+                    rhs=tok_codes[a][:].bitcast(FP8X4),
+                    rhs_scale=tok_plane[:, a * HALF : (a + 1) * HALF],
+                    start=True,
+                    stop=True,
+                )
+
+        gain = keep.tile([P, PACK], F32, name="gain")
+        nc.gpsimd.tensor_scalar(gain[:], gn_t, 0.5, 0.0, ALU.mult, ALU.add)
+        sg_bias = keep.tile([P, PACK], F32, name="sg_bias")
+        neg_th = keep.tile([P, PACK], F32, name="neg_th")
+        nc.gpsimd.tensor_scalar(neg_th[:], th_t, -1.0, 0.0, ALU.mult, ALU.add)
+        nc.gpsimd.tensor_tensor(sg_bias[:], neg_th[:], sl_t, ALU.mult)
+
+        def round_weight(name, raw):
+            rounded = keep.tile([P, PACK * N], BF16, name=name, align_bytes=64)
+            dst = rounded[:].rearrange("p (t m j) -> p t m j", t=PACK, j=PACK)
+            src = raw[:].rearrange("p j (m t) -> p t m j", t=PACK)
+            for a in range(2):
+                nc.gpsimd.tensor_scalar(dst[:, 2 * a : 2 * (a + 1)], src[:, 2 * a : 2 * (a + 1)], 1.0, 0.0, ALU.mult, ALU.add)
+            return rounded
+
+        def quantize(name, rounded, width):
+            codes = keep.tile([P, width], U32, name=name + "_codes", align_bytes=64)
+            plane = keep.tile([P, width], U8, name=name + "_plane", align_bytes=64)
+            nc.vector.quantize_mx(codes[:].bitcast(FP8X4), plane[:], rounded)
+            return codes, plane
+
+        w1_b = round_weight("w1_b", w1_raw)
+        w2_b = round_weight("w2_b", w2_raw)
+
+        s_rows = [keep.tile([P, S], F32, name=f"s_rows{t}") for t in range(PACK)]
+        ea = keep.tile([P, PACK, S], F32, name="ea")
+        for t in range(PACK):
+            top = keep.tile([P, 1], F32, name=f"top{t}")
+            nc.vector.tensor_scalar(s_rows[t][:], s_bank[t][:], 0.0625, None, ALU.mult, ALU.max, accum_out=top[:])
+            ea_bias = keep.tile([P, 1], F32, name=f"ea_bias{t}")
+            nc.vector.tensor_scalar(ea_bias[:], top[:], tau_t[:, t : t + 1], -1.0, ALU.mult, ALU.mult)
+            for a, part in enumerate(halves(n2_t)):
+                nc.scalar.activation(
+                    ea[:, t, a * HALF : (a + 1) * HALF],
+                    s_rows[t][:].indirect(part),
+                    ACT.Exp,
+                    bias=ea_bias[:],
+                    scale=tau_t[:, t : t + 1],
+                )
+        two_plane = keep.tile([P, S], U8, name="two_plane", align_bytes=64)
+        nc.vector.tensor_copy(two_plane[:], x_bytes[:].indirect(two_t[:]))
+        two_codes = keep.tile([P, S], U32, name="two_codes", align_bytes=64)
+        nc.vector.tensor_copy(two_codes[:], x_table[:].indirect(two_t[:]))
+        w1_codes, w1_plane = quantize("w1", w1_b[:], N)
+        w2_codes, w2_plane = quantize("w2", w2_b[:], N)
+
+        h_bank = [psum.tile([P, S], F32, name=f"h_bank{t}") for t in range(PACK)]
+        for t in range(PACK):
+            nc.tensor.matmul_mx(
+                h_bank[t][:],
+                lhsT=w2_codes[:, t * P : (t + 1) * P].bitcast(FP8X4),
+                lhsT_scale=w2_plane[:, t * P : (t + 1) * P],
+                rhs=two_codes[:].bitcast(FP8X4),
+                rhs_scale=two_plane[:],
+                start=True,
+                stop=False,
+            )
+
+        chunks = S // CHUNK
+        other = [keep.tile([P, S], F32, name=f"other{t}") for t in range(PACK)]
+        for t in range(PACK):
+            if t not in ACT_GATHERS:
+                for a, part in enumerate(halves(n1_t)):
+                    nc.vector.tensor_copy(other[t][:, a * HALF : (a + 1) * HALF], s_rows[t][:].indirect(part))
+        for c in range(chunks):
+            cols = slice(c * CHUNK, (c + 1) * CHUNK)
+            root = keep.tile([P, PACK, CHUNK], F32, name=f"root{c}")
+            nc.scalar.activation(root[:], ea[:, :, cols], ACT.Abs_reciprocal_sqrt, bias=0.25)
+            part = n1_t[:, c * CHUNK // 16 : (c + 1) * CHUNK // 16]
+            for t in ACT_GATHERS:
+                nc.scalar.activation(other[t][:, cols], s_rows[t][:].indirect(part), ACT.Copy)
+            factor = keep.tile([P, PACK, CHUNK], F32, name=f"factor{c}")
+            diff = keep.tile([P, PACK, CHUNK], F32, name=f"diff{c}")
+            for t in range(PACK):
+                nc.vector.scalar_tensor_tensor(factor[:, t, :], root[:, t, :], gain[:, t : t + 1], root[:, t, :], ALU.mult, ALU.mult)
+            for t in range(PACK):
+                nc.vector.scalar_tensor_tensor(diff[:, t, :], s_bank[t][:, cols], 0.0625, other[t][:, cols], ALU.mult, ALU.subtract)
+            z = keep.tile([P, CHUNK * PACK], BF16, name=f"z{c}", align_bytes=64)
+            nc.vector.tensor_tensor(
+                z[:].rearrange("p (a i t) -> p a t i", i=4, t=PACK),
+                diff[:].rearrange("p t (a i) -> p a t i", i=4),
+                factor[:].rearrange("p t (a i) -> p a t i", i=4),
+                ALU.mult,
+            )
+            z_codes, z_plane = quantize(f"z{c}", z[:], CHUNK)
+            for t in range(PACK):
+                nc.tensor.matmul_mx(
+                    h_bank[t][:, cols],
+                    lhsT=w1_codes[:, t * P : (t + 1) * P].bitcast(FP8X4),
+                    lhsT_scale=w1_plane[:, t * P : (t + 1) * P],
+                    rhs=z_codes[:].bitcast(FP8X4),
+                    rhs_scale=z_plane[:],
+                    start=False,
+                    stop=(c == chunks - 1),
+                )
+
+        out_rows = out.rearrange("(p t) n -> p t n", t=PACK)
+        h_rows = [keep.tile([P, S], F32, name=f"h_rows{t}") for t in range(PACK)]
+        for t in range(PACK):
+            nc.vector.tensor_copy(h_rows[t][:], h_bank[t][:])
+        for t in range(PACK):
+            for a, part in enumerate(halves(n3_t)):
+                cols = slice(a * HALF, (a + 1) * HALF)
+                sg = keep.tile([P, HALF], F32, name=f"sg{t}_{a}")
+                nc.scalar.activation(
+                    sg[:], h_rows[t][:].indirect(part), ACT.Sigmoid, bias=sg_bias[:, t : t + 1], scale=sl_t[:, t : t + 1]
+                )
+                result = keep.tile([P, HALF], F32, name=f"result{t}_{a}")
+                nc.vector.tensor_tensor(result[:], h_bank[t][:, cols], sg[:], ALU.mult)
+                nc.sync.dma_start(out_rows[:, t, cols], result[:])

@@ -19,7 +19,7 @@ P = 128
 PACK = 4
 HALF = S // 2
 CHUNK = 128
-ACT_GATHERS = (1, 2, 3)
+PIECES = ((0, 256), (256, 128), (384, 128))
 
 
 def tile_picked_kmixeraesa_none_p_kernel(
@@ -51,10 +51,8 @@ def tile_picked_kmixeraesa_none_p_kernel(
 
         d_bytes = keep.tile([P, G], U8, name="d_bytes", align_bytes=64)
         x_bytes = keep.tile([P, T], U8, name="x_bytes", align_bytes=64)
-        key_plane = keep.tile([P, H], U8, name="key_plane", align_bytes=64)
         nc.gpsimd.memset(d_bytes[:].bitcast(I32), 0)
         nc.vector.memset(x_bytes[:].bitcast(I32), 0)
-        nc.vector.memset(key_plane[:].bitcast(I32), 0)
 
         nc.gpsimd.dma_start(d_bytes[0:P:8, :].bitcast(I32), d_scales[0].bitcast(I32))
         k1_t = load_list("k1_t", k1)
@@ -63,24 +61,21 @@ def tile_picked_kmixeraesa_none_p_kernel(
             nc.scalar.dma_start(x_bytes[32 * q : 32 * q + 4, :].bitcast(I32), x_scales[0, 4 * q : 4 * q + 4, :].bitcast(I32))
         two_t = load_list("two_t", two)
         n2_t = load_list("n2_t", n2)
-        d_table = load_words("d_table", d_words)
         n1_t = load_list("n1_t", n1)
+        d_table = load_words("d_table", d_words)
         n3_t = load_list("n3_t", n3)
+        tau_t = keep.tile([P, PACK], F32, name="tau_t")
+        nc.sync.dma_start(tau_t[:], tau.rearrange("(p t) o -> p (t o)", t=PACK))
         x_table = load_words("x_table", x_words)
 
-        key_bytes = keep.tile([P, H], U8, name="key_bytes", tag="stage0", align_bytes=64)
+        key_bytes = keep.tile([P, H], U8, name="key_bytes", align_bytes=64)
         nc.vector.tensor_copy(key_bytes[:], d_bytes[:].indirect(k1_t[:]))
-        key_bytes_dealt = keep.tile([P, H], U8, name="key_bytes_dealt", tag="stage1", align_bytes=64)
+        key_plane = keep.tile([P, H], U8, name="key_plane", align_bytes=64)
         nc.vector.tensor_copy(
-            key_bytes_dealt[:].rearrange("p (t m) -> p m t", t=PACK), key_bytes[:].rearrange("p (m t) -> p m t", t=PACK)
+            key_plane[:].rearrange("p (t m) -> p m t", t=PACK), key_bytes[:].rearrange("p (m t) -> p m t", t=PACK)
         )
-        for r in range(4):
-            queue = nc.gpsimd if r == 0 else nc.scalar
-            queue.dma_start(key_plane[r:P:32, :].bitcast(I32), key_bytes_dealt[8 * r : P : 32, :].bitcast(I32))
-        columns = keep.tile([P, 32], F32, name="columns", tag="stage0", align_bytes=64)
-        tau_t, gn_t, sl_t, th_t = [columns[:, 8 * u : 8 * u + PACK] for u in range(4)]
-        for dst, src in ((tau_t, tau), (gn_t, gn), (sl_t, sl), (th_t, th)):
-            nc.gpsimd.dma_start(dst, src.rearrange("(p t) o -> p (t o)", t=PACK))
+        for r in range(1, 4):
+            nc.scalar.dma_start(key_plane[r:P:32, :].bitcast(I32), key_plane[8 * r : P : 32, :].bitcast(I32))
         key_words = keep.tile([P, H], U32, name="key_words", tag="stage2", align_bytes=64)
         nc.vector.tensor_copy(key_words[:], d_table[:].indirect(k1_t[:]))
         key_codes = keep.tile([P, H], U32, name="key_codes", align_bytes=64)
@@ -88,13 +83,18 @@ def tile_picked_kmixeraesa_none_p_kernel(
             key_codes[:].bitcast(I32).rearrange("p (t m) -> p m t", t=PACK),
             key_words[:].bitcast(I32).rearrange("p (m t) -> p m t", t=PACK),
         )
-        w1_raw = load_weight("w1_raw", w1, "stage2")
-        w2_raw = load_weight("w2_raw", w2, "stage1")
-        tok_plane = keep.tile([P, S], U8, name="tok_plane", align_bytes=64)
+        late = keep.tile([P, PACK * N + 32], F32, name="late", tag="d_table", align_bytes=64)
+        w2_raw = late[:, : PACK * N].rearrange("p (j n) -> p j n", j=PACK)
+        nc.sync.dma_start(w2_raw, w2.rearrange("(p j) n -> p j n", j=PACK))
+        w1_raw = load_weight("w1_raw", w1, "stage2")[:]
+        gn_t, sl_t, th_t = [late[:, PACK * N + 8 * u : PACK * N + 8 * u + PACK] for u in range(3)]
+        for dst, src in ((gn_t, gn), (sl_t, sl), (th_t, th)):
+            nc.sync.dma_start(dst, src.rearrange("(p t) o -> p (t o)", t=PACK))
+        tok_plane = keep.tile([P, S], U8, name="tok_plane", tag="token_plane", align_bytes=64)
         nc.vector.tensor_copy(tok_plane[:], x_bytes[:].indirect(offs_t[:]))
         tok_codes = []
         for a, part in enumerate(halves(offs_t)):
-            codes = keep.tile([P, HALF], U32, name=f"tok_codes{a}", align_bytes=64)
+            codes = keep.tile([P, HALF], U32, name=f"tok_codes{a}", tag=f"token_codes{a}", align_bytes=64)
             nc.vector.tensor_copy(codes[:], x_table[:].indirect(part))
             tok_codes.append(codes)
 
@@ -111,19 +111,11 @@ def tile_picked_kmixeraesa_none_p_kernel(
                     stop=True,
                 )
 
-        gain = keep.tile([P, PACK], F32, name="gain")
-        nc.gpsimd.tensor_scalar(gain[:], gn_t, 0.5, 0.0, ALU.mult, ALU.add)
-        sg_bias = keep.tile([P, PACK], F32, name="sg_bias")
-        neg_th = keep.tile([P, PACK], F32, name="neg_th")
-        nc.gpsimd.tensor_scalar(neg_th[:], th_t, -1.0, 0.0, ALU.mult, ALU.add)
-        nc.gpsimd.tensor_tensor(sg_bias[:], neg_th[:], sl_t, ALU.mult)
-
-        def round_weight(name, raw):
+        def round_weight(name, raw, copy):
             rounded = keep.tile([P, PACK * N], BF16, name=name, align_bytes=64)
-            dst = rounded[:].rearrange("p (t m j) -> p t m j", t=PACK, j=PACK)
-            src = raw[:].rearrange("p j (m t) -> p t m j", t=PACK)
-            for a in range(2):
-                nc.gpsimd.tensor_scalar(dst[:, 2 * a : 2 * (a + 1)], src[:, 2 * a : 2 * (a + 1)], 1.0, 0.0, ALU.mult, ALU.add)
+            copy(
+                rounded[:].rearrange("p (t m j) -> p m t j", t=PACK, j=PACK), raw.rearrange("p j (m t) -> p m t j", t=PACK)
+            )
             return rounded
 
         def quantize(name, rounded, width):
@@ -132,30 +124,43 @@ def tile_picked_kmixeraesa_none_p_kernel(
             nc.vector.quantize_mx(codes[:].bitcast(FP8X4), plane[:], rounded)
             return codes, plane
 
-        w1_b = round_weight("w1_b", w1_raw)
-        w2_b = round_weight("w2_b", w2_raw)
-
         s_rows = [keep.tile([P, S], F32, name=f"s_rows{t}") for t in range(PACK)]
-        ea = keep.tile([P, PACK, S], F32, name="ea")
-        for t in range(PACK):
-            top = keep.tile([P, 1], F32, name=f"top{t}")
-            nc.vector.tensor_scalar(s_rows[t][:], s_bank[t][:], 0.0625, None, ALU.mult, ALU.max, accum_out=top[:])
+        ea = [keep.tile([P, PACK, HALF], F32, name=f"ea{a}", tag=f"looked_up{a}") for a in range(2)]
+        top = [keep.tile([P, 1], F32, name=f"top{t}") for t in range(PACK)]
+
+        def leave_bank(t):
+            nc.vector.tensor_scalar(s_rows[t][:], s_bank[t][:], 0.0625, None, ALU.mult, ALU.max, accum_out=top[t][:])
+
+        def exponentials(t):
             ea_bias = keep.tile([P, 1], F32, name=f"ea_bias{t}")
-            nc.vector.tensor_scalar(ea_bias[:], top[:], tau_t[:, t : t + 1], -1.0, ALU.mult, ALU.mult)
+            nc.vector.tensor_scalar(ea_bias[:], top[t][:], tau_t[:, t : t + 1], -1.0, ALU.mult, ALU.mult)
             for a, part in enumerate(halves(n2_t)):
                 nc.scalar.activation(
-                    ea[:, t, a * HALF : (a + 1) * HALF],
+                    ea[a][:, t, :],
                     s_rows[t][:].indirect(part),
                     ACT.Exp,
                     bias=ea_bias[:],
                     scale=tau_t[:, t : t + 1],
                 )
-        two_plane = keep.tile([P, S], U8, name="two_plane", align_bytes=64)
+
+        leave_bank(0)
+        exponentials(0)
+        leave_bank(1)
+        for t in range(1, PACK):
+            if t + 1 < PACK:
+                leave_bank(t + 1)
+            exponentials(t)
+
+        two_plane = keep.tile([P, S], U8, name="two_plane", tag="token_plane", align_bytes=64)
         nc.vector.tensor_copy(two_plane[:], x_bytes[:].indirect(two_t[:]))
-        two_codes = keep.tile([P, S], U32, name="two_codes", align_bytes=64)
+        two_codes = keep.tile([P, S], U32, name="two_codes", tag="token_codes1", align_bytes=64)
         nc.vector.tensor_copy(two_codes[:], x_table[:].indirect(two_t[:]))
-        w1_codes, w1_plane = quantize("w1", w1_b[:], N)
+        w2_b = round_weight("w2_b", w2_raw, nc.vector.tensor_copy)
+        w1_b = round_weight("w1_b", w1_raw, nc.vector.tensor_copy)
         w2_codes, w2_plane = quantize("w2", w2_b[:], N)
+        w1_codes, w1_plane = quantize("w1", w1_b[:], N)
+        sg_bias = keep.tile([P, PACK], F32, name="sg_bias")
+        nc.vector.scalar_tensor_tensor(sg_bias[:], th_t, -1.0, sl_t, ALU.mult, ALU.mult)
 
         h_bank = [psum.tile([P, S], F32, name=f"h_bank{t}") for t in range(PACK)]
         for t in range(PACK):
@@ -169,43 +174,44 @@ def tile_picked_kmixeraesa_none_p_kernel(
                 stop=False,
             )
 
-        chunks = S // CHUNK
-        other = [keep.tile([P, S], F32, name=f"other{t}") for t in range(PACK)]
+        root = keep.tile([P, PACK, S], F32, name="root")
+        factor = keep.tile([P, PACK, S], F32, name="factor")
+        for a in range(2):
+            nc.scalar.activation(root[:, :, a * HALF : (a + 1) * HALF], ea[a][:], ACT.Abs_reciprocal_sqrt, bias=0.5, scale=2.0)
         for t in range(PACK):
-            if t not in ACT_GATHERS:
-                for a, part in enumerate(halves(n1_t)):
-                    nc.vector.tensor_copy(other[t][:, a * HALF : (a + 1) * HALF], s_rows[t][:].indirect(part))
-        for c in range(chunks):
-            cols = slice(c * CHUNK, (c + 1) * CHUNK)
-            root = keep.tile([P, PACK, CHUNK], F32, name=f"root{c}")
-            nc.scalar.activation(root[:], ea[:, :, cols], ACT.Abs_reciprocal_sqrt, bias=0.25)
-            part = n1_t[:, c * CHUNK // 16 : (c + 1) * CHUNK // 16]
-            for t in ACT_GATHERS:
-                nc.scalar.activation(other[t][:, cols], s_rows[t][:].indirect(part), ACT.Copy)
-            factor = keep.tile([P, PACK, CHUNK], F32, name=f"factor{c}")
-            diff = keep.tile([P, PACK, CHUNK], F32, name=f"diff{c}")
+            nc.vector.scalar_tensor_tensor(factor[:, t, :], root[:, t, :], gn_t[:, t : t + 1], root[:, t, :], ALU.mult, ALU.mult)
+        other = [keep.tile([P, PACK, HALF], F32, name=f"other{a}", tag=f"looked_up{a}") for a in range(2)]
+        for first, width in PIECES:
+            diff = keep.tile([P, PACK, width], F32, name=f"diff{first}")
+            part = n1_t[:, first // 16 : (first + width) // 16]
+            fetched = other[first // HALF][:, :, first % HALF : first % HALF + width]
             for t in range(PACK):
-                nc.vector.scalar_tensor_tensor(factor[:, t, :], root[:, t, :], gain[:, t : t + 1], root[:, t, :], ALU.mult, ALU.mult)
-            for t in range(PACK):
-                nc.vector.scalar_tensor_tensor(diff[:, t, :], s_bank[t][:, cols], 0.0625, other[t][:, cols], ALU.mult, ALU.subtract)
-            z = keep.tile([P, CHUNK * PACK], BF16, name=f"z{c}", align_bytes=64)
-            nc.vector.tensor_tensor(
-                z[:].rearrange("p (a i t) -> p a t i", i=4, t=PACK),
-                diff[:].rearrange("p t (a i) -> p a t i", i=4),
-                factor[:].rearrange("p t (a i) -> p a t i", i=4),
-                ALU.mult,
-            )
-            z_codes, z_plane = quantize(f"z{c}", z[:], CHUNK)
-            for t in range(PACK):
-                nc.tensor.matmul_mx(
-                    h_bank[t][:, cols],
-                    lhsT=w1_codes[:, t * P : (t + 1) * P].bitcast(FP8X4),
-                    lhsT_scale=w1_plane[:, t * P : (t + 1) * P],
-                    rhs=z_codes[:].bitcast(FP8X4),
-                    rhs_scale=z_plane[:],
-                    start=False,
-                    stop=(c == chunks - 1),
+                nc.scalar.activation(fetched[:, t, :], s_rows[t][:].indirect(part), ACT.Copy)
+                nc.vector.scalar_tensor_tensor(
+                    diff[:, t, :], s_bank[t][:, first : first + width], 0.0625, fetched[:, t, :], ALU.mult, ALU.subtract
                 )
+            zs = []
+            for begin in range(first, first + width, CHUNK):
+                z = keep.tile([P, CHUNK * PACK], BF16, name=f"z{begin}", align_bytes=64)
+                nc.vector.tensor_tensor(
+                    z[:].rearrange("p (a i t) -> p a t i", i=4, t=PACK),
+                    diff[:, :, begin - first : begin - first + CHUNK].rearrange("p t (a i) -> p a t i", i=4),
+                    factor[:, :, begin : begin + CHUNK].rearrange("p t (a i) -> p a t i", i=4),
+                    ALU.mult,
+                )
+                zs.append((begin, z))
+            for begin, z in zs:
+                z_codes, z_plane = quantize(f"z{begin}", z[:], CHUNK)
+                for t in range(PACK):
+                    nc.tensor.matmul_mx(
+                        h_bank[t][:, begin : begin + CHUNK],
+                        lhsT=w1_codes[:, t * P : (t + 1) * P].bitcast(FP8X4),
+                        lhsT_scale=w1_plane[:, t * P : (t + 1) * P],
+                        rhs=z_codes[:].bitcast(FP8X4),
+                        rhs_scale=z_plane[:],
+                        start=False,
+                        stop=(begin + CHUNK == S),
+                    )
 
         out_rows = out.rearrange("(p t) n -> p t n", t=PACK)
         h_rows = [keep.tile([P, S], F32, name=f"h_rows{t}") for t in range(PACK)]

@@ -18,8 +18,7 @@ ACT = mybir.ActivationFunctionType
 P = 128
 PACK = 4
 HALF = S // 2
-CHUNK = 128
-PIECES = ((0, 256), (256, 128), (384, 128))
+Z_WIDTHS = (256, 128)
 
 
 def tile_picked_kmixeraesa_none_p_kernel(
@@ -51,31 +50,31 @@ def tile_picked_kmixeraesa_none_p_kernel(
 
         d_bytes = keep.tile([P, G], U8, name="d_bytes", align_bytes=64)
         x_bytes = keep.tile([P, T], U8, name="x_bytes", align_bytes=64)
-        nc.gpsimd.memset(d_bytes[:].bitcast(I32), 0)
-        nc.vector.memset(x_bytes[:].bitcast(I32), 0)
+        nc.vector.memset(d_bytes[:].bitcast(I32), 0)
+        nc.gpsimd.memset(x_bytes[:].bitcast(I32), 0)
 
-        nc.gpsimd.dma_start(d_bytes[0:P:8, :].bitcast(I32), d_scales[0].bitcast(I32))
         k1_t = load_list("k1_t", k1)
         offs_t = load_list("offs_t", offs)
-        for q in range(4):
-            nc.scalar.dma_start(x_bytes[32 * q : 32 * q + 4, :].bitcast(I32), x_scales[0, 4 * q : 4 * q + 4, :].bitcast(I32))
         two_t = load_list("two_t", two)
         n2_t = load_list("n2_t", n2)
         n1_t = load_list("n1_t", n1)
-        d_table = load_words("d_table", d_words)
         n3_t = load_list("n3_t", n3)
+        nc.sync.dma_start(d_bytes[0:P:8, :].bitcast(I32), d_scales[0].bitcast(I32))
+        d_table = load_words("d_table", d_words)
+        for q in range(4):
+            nc.sync.dma_start(x_bytes[32 * q : 32 * q + 4, :].bitcast(I32), x_scales[0, 4 * q : 4 * q + 4, :].bitcast(I32))
+        x_table = load_words("x_table", x_words)
         tau_t = keep.tile([P, PACK], F32, name="tau_t")
         nc.sync.dma_start(tau_t[:], tau.rearrange("(p t) o -> p (t o)", t=PACK))
-        x_table = load_words("x_table", x_words)
 
-        key_bytes = keep.tile([P, H], U8, name="key_bytes", align_bytes=64)
+        key_bytes = keep.tile([P, H], U8, name="key_bytes", tag="stage1", align_bytes=64)
         nc.vector.tensor_copy(key_bytes[:], d_bytes[:].indirect(k1_t[:]))
         key_plane = keep.tile([P, H], U8, name="key_plane", align_bytes=64)
         nc.vector.tensor_copy(
             key_plane[:].rearrange("p (t m) -> p m t", t=PACK), key_bytes[:].rearrange("p (m t) -> p m t", t=PACK)
         )
         for r in range(1, 4):
-            nc.scalar.dma_start(key_plane[r:P:32, :].bitcast(I32), key_plane[8 * r : P : 32, :].bitcast(I32))
+            nc.sync.dma_start(key_plane[r:P:32, :].bitcast(I32), key_plane[8 * r : P : 32, :].bitcast(I32))
         key_words = keep.tile([P, H], U32, name="key_words", tag="stage2", align_bytes=64)
         nc.vector.tensor_copy(key_words[:], d_table[:].indirect(k1_t[:]))
         key_codes = keep.tile([P, H], U32, name="key_codes", align_bytes=64)
@@ -83,9 +82,10 @@ def tile_picked_kmixeraesa_none_p_kernel(
             key_codes[:].bitcast(I32).rearrange("p (t m) -> p m t", t=PACK),
             key_words[:].bitcast(I32).rearrange("p (m t) -> p m t", t=PACK),
         )
-        late = keep.tile([P, PACK * N + 32], F32, name="late", tag="d_table", align_bytes=64)
-        w2_raw = late[:, : PACK * N].rearrange("p (j n) -> p j n", j=PACK)
-        nc.sync.dma_start(w2_raw, w2.rearrange("(p j) n -> p j n", j=PACK))
+        late = keep.tile([P, PACK * N + 32], F32, name="late", tag="stage1", align_bytes=64)
+        w2_raw = late[:, : PACK * N].rearrange("p (a j n) -> p a j n", a=2, j=PACK)
+        for a in range(2):
+            nc.sync.dma_start(w2_raw[:, a], w2.rearrange("(p j) n -> p j n", j=PACK)[:, :, a * HALF : (a + 1) * HALF])
         w1_raw = load_weight("w1_raw", w1, "stage2")[:]
         gn_t, sl_t, th_t = [late[:, PACK * N + 8 * u : PACK * N + 8 * u + PACK] for u in range(3)]
         for dst, src in ((gn_t, gn), (sl_t, sl), (th_t, th)):
@@ -124,6 +124,15 @@ def tile_picked_kmixeraesa_none_p_kernel(
             nc.vector.quantize_mx(codes[:].bitcast(FP8X4), plane[:], rounded)
             return codes, plane
 
+        w2_b = keep.tile([P, PACK * N], BF16, name="w2_b", align_bytes=64)
+
+        def round_w2(a, copy):
+            copy(
+                w2_b[:].rearrange("p (t m j) -> p m t j", t=PACK, j=PACK)[:, 64 * a : 64 * (a + 1)],
+                w2_raw[:, a].rearrange("p j (m t) -> p m t j", t=PACK),
+            )
+
+        round_w2(0, nc.scalar.copy)
         s_rows = [keep.tile([P, S], F32, name=f"s_rows{t}") for t in range(PACK)]
         ea = [keep.tile([P, PACK, HALF], F32, name=f"ea{a}", tag=f"looked_up{a}") for a in range(2)]
         top = [keep.tile([P, 1], F32, name=f"top{t}") for t in range(PACK)]
@@ -155,7 +164,7 @@ def tile_picked_kmixeraesa_none_p_kernel(
         nc.vector.tensor_copy(two_plane[:], x_bytes[:].indirect(two_t[:]))
         two_codes = keep.tile([P, S], U32, name="two_codes", tag="token_codes1", align_bytes=64)
         nc.vector.tensor_copy(two_codes[:], x_table[:].indirect(two_t[:]))
-        w2_b = round_weight("w2_b", w2_raw, nc.vector.tensor_copy)
+        round_w2(1, nc.vector.tensor_copy)
         w1_b = round_weight("w1_b", w1_raw, nc.vector.tensor_copy)
         w2_codes, w2_plane = quantize("w2", w2_b[:], N)
         w1_codes, w1_plane = quantize("w1", w1_b[:], N)
@@ -163,6 +172,10 @@ def tile_picked_kmixeraesa_none_p_kernel(
         nc.vector.scalar_tensor_tensor(sg_bias[:], th_t, -1.0, sl_t, ALU.mult, ALU.mult)
 
         h_bank = [psum.tile([P, S], F32, name=f"h_bank{t}") for t in range(PACK)]
+
+        def h_part(t, a):
+            return h_bank[t][:, a * HALF : (a + 1) * HALF]
+
         for t in range(PACK):
             nc.tensor.matmul_mx(
                 h_bank[t][:],
@@ -174,56 +187,64 @@ def tile_picked_kmixeraesa_none_p_kernel(
                 stop=False,
             )
 
-        root = keep.tile([P, PACK, S], F32, name="root")
-        factor = keep.tile([P, PACK, S], F32, name="factor")
+        factor = []
         for a in range(2):
-            nc.scalar.activation(root[:, :, a * HALF : (a + 1) * HALF], ea[a][:], ACT.Abs_reciprocal_sqrt, bias=0.5, scale=2.0)
-        for t in range(PACK):
-            nc.vector.scalar_tensor_tensor(factor[:, t, :], root[:, t, :], gn_t[:, t : t + 1], root[:, t, :], ALU.mult, ALU.mult)
-        other = [keep.tile([P, PACK, HALF], F32, name=f"other{a}", tag=f"looked_up{a}") for a in range(2)]
-        for first, width in PIECES:
-            diff = keep.tile([P, PACK, width], F32, name=f"diff{first}")
-            part = n1_t[:, first // 16 : (first + width) // 16]
-            fetched = other[first // HALF][:, :, first % HALF : first % HALF + width]
+            root = keep.tile([P, PACK, HALF], F32, name=f"root{a}")
+            nc.scalar.activation(root[:], ea[a][:], ACT.Abs_reciprocal_sqrt, bias=0.5, scale=2.0)
+            factor.append(keep.tile([P, PACK, HALF], F32, name=f"factor{a}"))
             for t in range(PACK):
-                nc.scalar.activation(fetched[:, t, :], s_rows[t][:].indirect(part), ACT.Copy)
                 nc.vector.scalar_tensor_tensor(
-                    diff[:, t, :], s_bank[t][:, first : first + width], 0.0625, fetched[:, t, :], ALU.mult, ALU.subtract
+                    factor[a][:, t, :], root[:, t, :], gn_t[:, t : t + 1], root[:, t, :], ALU.mult, ALU.mult
                 )
+        other = [keep.tile([P, PACK, HALF], F32, name=f"other{a}", tag=f"looked_up{a}") for a in range(2)]
+        h_rows = [keep.tile([P, S], F32, name=f"h_rows{t}") for t in range(PACK)]
+        for a, part in enumerate(halves(n1_t)):
+            diff = keep.tile([P, PACK, HALF], F32, name=f"diff{a}")
+            for t in range(PACK):
+                nc.scalar.activation(other[a][:, t, :], s_rows[t][:].indirect(part), ACT.Copy)
+                nc.vector.scalar_tensor_tensor(
+                    diff[:, t, :], s_bank[t][:, a * HALF : (a + 1) * HALF], 0.0625, other[a][:, t, :], ALU.mult, ALU.subtract
+                )
+            width = Z_WIDTHS[a]
             zs = []
-            for begin in range(first, first + width, CHUNK):
-                z = keep.tile([P, CHUNK * PACK], BF16, name=f"z{begin}", align_bytes=64)
+            for begin in range(0, HALF, width):
+                z = keep.tile([P, width * PACK], BF16, name=f"z{a}_{begin}", align_bytes=64)
                 nc.vector.tensor_tensor(
                     z[:].rearrange("p (a i t) -> p a t i", i=4, t=PACK),
-                    diff[:, :, begin - first : begin - first + CHUNK].rearrange("p t (a i) -> p a t i", i=4),
-                    factor[:, :, begin : begin + CHUNK].rearrange("p t (a i) -> p a t i", i=4),
+                    diff[:, :, begin : begin + width].rearrange("p t (a i) -> p a t i", i=4),
+                    factor[a][:, :, begin : begin + width].rearrange("p t (a i) -> p a t i", i=4),
                     ALU.mult,
                 )
                 zs.append((begin, z))
             for begin, z in zs:
-                z_codes, z_plane = quantize(f"z{begin}", z[:], CHUNK)
+                z_codes, z_plane = quantize(f"z{a}_{begin}", z[:], width)
                 for t in range(PACK):
                     nc.tensor.matmul_mx(
-                        h_bank[t][:, begin : begin + CHUNK],
+                        h_part(t, a)[:, begin : begin + width],
                         lhsT=w1_codes[:, t * P : (t + 1) * P].bitcast(FP8X4),
                         lhsT_scale=w1_plane[:, t * P : (t + 1) * P],
                         rhs=z_codes[:].bitcast(FP8X4),
                         rhs_scale=z_plane[:],
                         start=False,
-                        stop=(begin + CHUNK == S),
+                        stop=(a == 1 and begin + width == HALF),
                     )
-
-        out_rows = out.rearrange("(p t) n -> p t n", t=PACK)
-        h_rows = [keep.tile([P, S], F32, name=f"h_rows{t}") for t in range(PACK)]
         for t in range(PACK):
             nc.vector.tensor_copy(h_rows[t][:], h_bank[t][:])
+
+        out_rows = out.rearrange("(p t) n -> p t n", t=PACK)
         for t in range(PACK):
-            for a, part in enumerate(halves(n3_t)):
-                cols = slice(a * HALF, (a + 1) * HALF)
-                sg = keep.tile([P, HALF], F32, name=f"sg{t}_{a}")
+            width = HALF if t + 1 < PACK else HALF // 2
+            for begin in [0, HALF] if t + 1 < PACK else [0, HALF, HALF + HALF // 2]:
+                width = HALF if (t + 1 < PACK or begin == 0) else HALF // 2
+                sg = keep.tile([P, width], F32, name=f"sg{t}_{begin}")
                 nc.scalar.activation(
-                    sg[:], h_rows[t][:].indirect(part), ACT.Sigmoid, bias=sg_bias[:, t : t + 1], scale=sl_t[:, t : t + 1]
+                    sg[:],
+                    h_rows[t][:].indirect(n3_t[:, begin // 16 : (begin + width) // 16]),
+                    ACT.Sigmoid,
+                    bias=sg_bias[:, t : t + 1],
+                    scale=sl_t[:, t : t + 1],
                 )
-                result = keep.tile([P, HALF], F32, name=f"result{t}_{a}")
-                nc.vector.tensor_tensor(result[:], h_bank[t][:, cols], sg[:], ALU.mult)
-                nc.sync.dma_start(out_rows[:, t, cols], result[:])
+                result = keep.tile([P, width], F32, name=f"result{t}_{begin}")
+                at = begin % HALF
+                nc.vector.tensor_tensor(result[:], h_part(t, begin // HALF)[:, at : at + width], sg[:], ALU.mult)
+                nc.sync.dma_start(out_rows[:, t, begin : begin + width], result[:])

@@ -18,7 +18,7 @@ ACT = mybir.ActivationFunctionType
 P = 128
 PACK = 4
 HALF = S // 2
-Z_WIDTHS = (256, 128)
+PIECES = ((0, 256), (256, 128), (384, 128))
 
 
 def tile_picked_kmixeraesa_none_p_kernel(
@@ -99,8 +99,8 @@ def tile_picked_kmixeraesa_none_p_kernel(
             tok_codes.append(codes)
 
         s_bank = [psum.tile([P, S], F32, name=f"s_bank{t}") for t in range(PACK)]
-        for a in range(2):
-            for t in range(PACK):
+        for t in range(PACK):
+            for a in range(2):
                 nc.tensor.matmul_mx(
                     s_bank[t][:, a * HALF : (a + 1) * HALF],
                     lhsT=key_codes[:, t * P : (t + 1) * P].bitcast(FP8X4),
@@ -111,24 +111,18 @@ def tile_picked_kmixeraesa_none_p_kernel(
                     stop=True,
                 )
 
-        def round_weight(name, raw, copy):
-            rounded = keep.tile([P, PACK * N], BF16, name=name, align_bytes=64)
-            copy(
-                rounded[:].rearrange("p (t m j) -> p m t j", t=PACK, j=PACK), raw.rearrange("p j (m t) -> p m t j", t=PACK)
-            )
-            return rounded
-
         def quantize(name, rounded, width):
             codes = keep.tile([P, width], U32, name=name + "_codes", align_bytes=64)
             plane = keep.tile([P, width], U8, name=name + "_plane", align_bytes=64)
             nc.vector.quantize_mx(codes[:].bitcast(FP8X4), plane[:], rounded)
             return codes, plane
 
-        w2_b = keep.tile([P, PACK * N], BF16, name="w2_b", align_bytes=64)
+        w_b = keep.tile([P, 2 * PACK * N], BF16, name="w_b", align_bytes=64)
+        w1_b, w2_b = w_b[:, : PACK * N], w_b[:, PACK * N :]
 
         def round_w2(a, copy):
             copy(
-                w2_b[:].rearrange("p (t m j) -> p m t j", t=PACK, j=PACK)[:, 64 * a : 64 * (a + 1)],
+                w2_b.rearrange("p (t m j) -> p m t j", t=PACK, j=PACK)[:, 64 * a : 64 * (a + 1)],
                 w2_raw[:, a].rearrange("p j (m t) -> p m t j", t=PACK),
             )
 
@@ -165,9 +159,11 @@ def tile_picked_kmixeraesa_none_p_kernel(
         two_codes = keep.tile([P, S], U32, name="two_codes", tag="token_codes1", align_bytes=64)
         nc.vector.tensor_copy(two_codes[:], x_table[:].indirect(two_t[:]))
         round_w2(1, nc.vector.tensor_copy)
-        w1_b = round_weight("w1_b", w1_raw, nc.vector.tensor_copy)
-        w2_codes, w2_plane = quantize("w2", w2_b[:], N)
-        w1_codes, w1_plane = quantize("w1", w1_b[:], N)
+        nc.vector.tensor_copy(
+            w1_b.rearrange("p (t m j) -> p m t j", t=PACK, j=PACK), w1_raw.rearrange("p j (m t) -> p m t j", t=PACK)
+        )
+        w_codes, w_plane = quantize("w", w_b[:], 2 * N)
+        w1_codes, w2_codes, w1_plane, w2_plane = w_codes[:, :N], w_codes[:, N:], w_plane[:, :N], w_plane[:, N:]
         sg_bias = keep.tile([P, PACK], F32, name="sg_bias")
         nc.vector.scalar_tensor_tensor(sg_bias[:], th_t, -1.0, sl_t, ALU.mult, ALU.mult)
 
@@ -198,36 +194,33 @@ def tile_picked_kmixeraesa_none_p_kernel(
                 )
         other = [keep.tile([P, PACK, HALF], F32, name=f"other{a}", tag=f"looked_up{a}") for a in range(2)]
         h_rows = [keep.tile([P, S], F32, name=f"h_rows{t}") for t in range(PACK)]
-        for a, part in enumerate(halves(n1_t)):
-            diff = keep.tile([P, PACK, HALF], F32, name=f"diff{a}")
+        for first, width in PIECES:
+            a, at = divmod(first, HALF)
+            diff = keep.tile([P, PACK, width], F32, name=f"diff{first}")
             for t in range(PACK):
-                nc.scalar.activation(other[a][:, t, :], s_rows[t][:].indirect(part), ACT.Copy)
+                fetched = other[a][:, t, at : at + width]
+                nc.scalar.activation(fetched, s_rows[t][:].indirect(n1_t[:, first // 16 : (first + width) // 16]), ACT.Copy)
                 nc.vector.scalar_tensor_tensor(
-                    diff[:, t, :], s_bank[t][:, a * HALF : (a + 1) * HALF], 0.0625, other[a][:, t, :], ALU.mult, ALU.subtract
+                    diff[:, t, :], s_bank[t][:, first : first + width], 0.0625, fetched, ALU.mult, ALU.subtract
                 )
-            width = Z_WIDTHS[a]
-            zs = []
-            for begin in range(0, HALF, width):
-                z = keep.tile([P, width * PACK], BF16, name=f"z{a}_{begin}", align_bytes=64)
-                nc.vector.tensor_tensor(
-                    z[:].rearrange("p (a i t) -> p a t i", i=4, t=PACK),
-                    diff[:, :, begin : begin + width].rearrange("p t (a i) -> p a t i", i=4),
-                    factor[a][:, :, begin : begin + width].rearrange("p t (a i) -> p a t i", i=4),
-                    ALU.mult,
+            z = keep.tile([P, width * PACK], BF16, name=f"z{first}", align_bytes=64)
+            nc.vector.tensor_tensor(
+                z[:].rearrange("p (a i t) -> p a t i", i=4, t=PACK),
+                diff[:].rearrange("p t (a i) -> p a t i", i=4),
+                factor[a][:, :, at : at + width].rearrange("p t (a i) -> p a t i", i=4),
+                ALU.mult,
+            )
+            z_codes, z_plane = quantize(f"z{first}", z[:], width)
+            for t in range(PACK):
+                nc.tensor.matmul_mx(
+                    h_bank[t][:, first : first + width],
+                    lhsT=w1_codes[:, t * P : (t + 1) * P].bitcast(FP8X4),
+                    lhsT_scale=w1_plane[:, t * P : (t + 1) * P],
+                    rhs=z_codes[:].bitcast(FP8X4),
+                    rhs_scale=z_plane[:],
+                    start=False,
+                    stop=(first + width == S),
                 )
-                zs.append((begin, z))
-            for begin, z in zs:
-                z_codes, z_plane = quantize(f"z{a}_{begin}", z[:], width)
-                for t in range(PACK):
-                    nc.tensor.matmul_mx(
-                        h_part(t, a)[:, begin : begin + width],
-                        lhsT=w1_codes[:, t * P : (t + 1) * P].bitcast(FP8X4),
-                        lhsT_scale=w1_plane[:, t * P : (t + 1) * P],
-                        rhs=z_codes[:].bitcast(FP8X4),
-                        rhs_scale=z_plane[:],
-                        start=False,
-                        stop=(a == 1 and begin + width == HALF),
-                    )
         for t in range(PACK):
             nc.vector.tensor_copy(h_rows[t][:], h_bank[t][:])
 

from contextlib import ExitStack

import concourse.mybir as mybir

K, T, S, N, G, H = 512, 2048, 512, 512, 2048, 512
FLOPS = 3 * 2 * 512 * 512 * 512

F32 = mybir.dt.float32
BF16 = mybir.dt.bfloat16
I32 = mybir.dt.int32
U32 = mybir.dt.uint32
U16 = mybir.dt.uint16
U8 = mybir.dt.uint8
FP8X4 = mybir.dt.float8_e4m3fn_x4
ALU = mybir.AluOpType
ACT = mybir.ActivationFunctionType

P = 128
PACK = 4
HALF = S // 2
PIECES = ((0, 256), (256, 128), (384, 128))


def tile_picked_kmixeraesa_none_p_kernel(
    tc, x_words, x_scales, d_words, d_scales, tau, gn, w1, w2, sl, th, offs, k1, n1, n2, two, n3, out
):
    nc = tc.nc
    with ExitStack() as ctx:
        keep = ctx.enter_context(tc.tile_pool(name="keep", bufs=1))
        psum = ctx.enter_context(tc.psum_pool(name="psum", bufs=1))

        def load_list(name, src):
            tile = keep.tile([P, S // 16], U16, name=name)
            nc.sync.dma_start(tile[:], src)
            return tile

        def load_words(name, src):
            tile = keep.tile([P, T], U32, name=name, align_bytes=64)
            nc.sync.dma_start(tile[:].bitcast(I32), src[0].rearrange("p n t -> p (n t)").bitcast(I32))
            return tile


        def load_weight(name, src, tag):
            tile = keep.tile([P, PACK, N], F32, name=name, tag=tag, align_bytes=64)
            nc.sync.dma_start(tile[:], src.rearrange("(p j) n -> p j n", j=PACK))
            return tile

        def halves(lst):
            return [lst[:, 16 * a : 16 * (a + 1)] for a in range(2)]

        d_bytes = keep.tile([P, G], U8, name="d_bytes", align_bytes=64)
        x_bytes = keep.tile([P, T], U8, name="x_bytes", align_bytes=64)
        nc.vector.memset(d_bytes[:].bitcast(I32), 0)
        nc.gpsimd.memset(x_bytes[:].bitcast(I32), 0)

        k1_t = load_list("k1_t", k1)
        offs_t = load_list("offs_t", offs)
        two_t = load_list("two_t", two)
        n2_t = load_list("n2_t", n2)
        n1_t = load_list("n1_t", n1)
        n3_t = load_list("n3_t", n3)
        nc.sync.dma_start(d_bytes[0:P:8, :].bitcast(I32), d_scales[0].bitcast(I32))
        d_table = load_words("d_table", d_words)
        for q in range(4):
            nc.sync.dma_start(x_bytes[32 * q : 32 * q + 4, :].bitcast(I32), x_scales[0, 4 * q : 4 * q + 4, :].bitcast(I32))
        x_table = load_words("x_table", x_words)
        tau_t = keep.tile([P, PACK], F32, name="tau_t")
        nc.sync.dma_start(tau_t[:], tau.rearrange("(p t) o -> p (t o)", t=PACK))

        key_bytes = keep.tile([P, H], U8, name="key_bytes", tag="stage1", align_bytes=64)
        nc.vector.tensor_copy(key_bytes[:], d_bytes[:].indirect(k1_t[:]))
        key_plane = keep.tile([P, H], U8, name="key_plane", align_bytes=64)
        nc.vector.tensor_copy(
            key_plane[:].rearrange("p (t m) -> p m t", t=PACK), key_bytes[:].rearrange("p (m t) -> p m t", t=PACK)
        )
        for r in range(1, 4):
            nc.sync.dma_start(key_plane[r:P:32, :].bitcast(I32), key_plane[8 * r : P : 32, :].bitcast(I32))
        key_words = keep.tile([P, H], U32, name="key_words", tag="stage2", align_bytes=64)
        nc.vector.tensor_copy(key_words[:], d_table[:].indirect(k1_t[:]))
        key_codes = keep.tile([P, H], U32, name="key_codes", align_bytes=64)
        nc.vector.tensor_copy(
            key_codes[:].bitcast(I32).rearrange("p (t m) -> p m t", t=PACK),
            key_words[:].bitcast(I32).rearrange("p (m t) -> p m t", t=PACK),
        )
        late = keep.tile([P, PACK * N + 32], F32, name="late", tag="stage1", align_bytes=64)
        w2_raw = late[:, : PACK * N].rearrange("p (a j n) -> p a j n", a=2, j=PACK)
        for a in range(2):
            nc.sync.dma_start(w2_raw[:, a], w2.rearrange("(p j) n -> p j n", j=PACK)[:, :, a * HALF : (a + 1) * HALF])
        w1_raw = load_weight("w1_raw", w1, "stage2")[:]
        gn_t, sl_t, th_t = [late[:, PACK * N + 8 * u : PACK * N + 8 * u + PACK] for u in range(3)]
        for dst, src in ((gn_t, gn), (sl_t, sl), (th_t, th)):
            nc.sync.dma_start(dst, src.rearrange("(p t) o -> p (t o)", t=PACK))
        tok_plane = keep.tile([P, S], U8, name="tok_plane", tag="token_plane", align_bytes=64)
        nc.vector.tensor_copy(tok_plane[:], x_bytes[:].indirect(offs_t[:]))
        tok_codes = []
        for a, part in enumerate(halves(offs_t)):
            codes = keep.tile([P, HALF], U32, name=f"tok_codes{a}", tag=f"token_codes{a}", align_bytes=64)
            nc.vector.tensor_copy(codes[:], x_table[:].indirect(part))
            tok_codes.append(codes)

        s_bank = [psum.tile([P, S], F32, name=f"s_bank{t}") for t in range(PACK)]
        for t in range(PACK):
            for a in range(2):
                nc.tensor.matmul_mx(
                    s_bank[t][:, a * HALF : (a + 1) * HALF],
                    lhsT=key_codes[:, t * P : (t + 1) * P].bitcast(FP8X4),
                    lhsT_scale=key_plane[:, t * P : (t + 1) * P],
                    rhs=tok_codes[a][:].bitcast(FP8X4),
                    rhs_scale=tok_plane[:, a * HALF : (a + 1) * HALF],
                    start=True,
                    stop=True,
                )

        def quantize(name, rounded, width):
            codes = keep.tile([P, width], U32, name=name + "_codes", align_bytes=64)
            plane = keep.tile([P, width], U8, name=name + "_plane", align_bytes=64)
            nc.vector.quantize_mx(codes[:].bitcast(FP8X4), plane[:], rounded)
            return codes, plane

        w_b = keep.tile([P, 2 * PACK * N], BF16, name="w_b", align_bytes=64)
        w1_b, w2_b = w_b[:, : PACK * N], w_b[:, PACK * N :]

        def round_w2(a, copy):
            copy(
                w2_b.rearrange("p (t m j) -> p m t j", t=PACK, j=PACK)[:, 64 * a : 64 * (a + 1)],
                w2_raw[:, a].rearrange("p j (m t) -> p m t j", t=PACK),
            )

        round_w2(0, nc.scalar.copy)
        s_rows = [keep.tile([P, S], F32, name=f"s_rows{t}") for t in range(PACK)]
        ea = [keep.tile([P, PACK, HALF], F32, name=f"ea{a}", tag=f"looked_up{a}") for a in range(2)]
        top = [keep.tile([P, 1], F32, name=f"top{t}") for t in range(PACK)]

        def leave_bank(t):
            nc.vector.tensor_scalar(s_rows[t][:], s_bank[t][:], 0.0625, None, ALU.mult, ALU.max, accum_out=top[t][:])

        def exponentials(t):
            ea_bias = keep.tile([P, 1], F32, name=f"ea_bias{t}")
            nc.vector.tensor_scalar(ea_bias[:], top[t][:], tau_t[:, t : t + 1], -1.0, ALU.mult, ALU.mult)
            for a, part in enumerate(halves(n2_t)):
                nc.scalar.activation(
                    ea[a][:, t, :],
                    s_rows[t][:].indirect(part),
                    ACT.Exp,
                    bias=ea_bias[:],
                    scale=tau_t[:, t : t + 1],
                )

        leave_bank(0)
        exponentials(0)
        leave_bank(1)
        for t in range(1, PACK):
            if t + 1 < PACK:
                leave_bank(t + 1)
            exponentials(t)

        two_plane = keep.tile([P, S], U8, name="two_plane", tag="token_plane", align_bytes=64)
        nc.vector.tensor_copy(two_plane[:], x_bytes[:].indirect(two_t[:]))
        two_codes = keep.tile([P, S], U32, name="two_codes", tag="token_codes1", align_bytes=64)
        nc.vector.tensor_copy(two_codes[:], x_table[:].indirect(two_t[:]))
        round_w2(1, nc.vector.tensor_copy)
        nc.vector.tensor_copy(
            w1_b.rearrange("p (t m j) -> p m t j", t=PACK, j=PACK), w1_raw.rearrange("p j (m t) -> p m t j", t=PACK)
        )
        w_codes, w_plane = quantize("w", w_b[:], 2 * N)
        w1_codes, w2_codes, w1_plane, w2_plane = w_codes[:, :N], w_codes[:, N:], w_plane[:, :N], w_plane[:, N:]
        sg_bias = keep.tile([P, PACK], F32, name="sg_bias")
        nc.vector.scalar_tensor_tensor(sg_bias[:], th_t, -1.0, sl_t, ALU.mult, ALU.mult)

        h_bank = [psum.tile([P, S], F32, name=f"h_bank{t}") for t in range(PACK)]

        def h_part(t, a):
            return h_bank[t][:, a * HALF : (a + 1) * HALF]

        for t in range(PACK):
            nc.tensor.matmul_mx(
                h_bank[t][:],
                lhsT=w2_codes[:, t * P : (t + 1) * P].bitcast(FP8X4),
                lhsT_scale=w2_plane[:, t * P : (t + 1) * P],
                rhs=two_codes[:].bitcast(FP8X4),
                rhs_scale=two_plane[:],
                start=True,
                stop=False,
            )

        factor = []
        for a in range(2):
            root = keep.tile([P, PACK, HALF], F32, name=f"root{a}")
            nc.scalar.activation(root[:], ea[a][:], ACT.Abs_reciprocal_sqrt, bias=0.5, scale=2.0)
            factor.append(keep.tile([P, PACK, HALF], F32, name=f"factor{a}"))
            for t in range(PACK):
                nc.vector.scalar_tensor_tensor(
                    factor[a][:, t, :], root[:, t, :], gn_t[:, t : t + 1], root[:, t, :], ALU.mult, ALU.mult
                )
        other = [keep.tile([P, PACK, HALF], F32, name=f"other{a}", tag=f"looked_up{a}") for a in range(2)]
        h_rows = [keep.tile([P, S], F32, name=f"h_rows{t}") for t in range(PACK)]
        for first, width in PIECES:
            a, at = divmod(first, HALF)
            diff = keep.tile([P, PACK, width], F32, name=f"diff{first}")
            for t in range(PACK):
                fetched = other[a][:, t, at : at + width]
                nc.scalar.activation(fetched, s_rows[t][:].indirect(n1_t[:, first // 16 : (first + width) // 16]), ACT.Copy)
                nc.vector.scalar_tensor_tensor(
                    diff[:, t, :], s_bank[t][:, first : first + width], 0.0625, fetched, ALU.mult, ALU.subtract
                )
            z = keep.tile([P, width * PACK], BF16, name=f"z{first}", align_bytes=64)
            nc.vector.tensor_tensor(
                z[:].rearrange("p (a i t) -> p a t i", i=4, t=PACK),
                diff[:].rearrange("p t (a i) -> p a t i", i=4),
                factor[a][:, :, at : at + width].rearrange("p t (a i) -> p a t i", i=4),
                ALU.mult,
            )
            z_codes, z_plane = quantize(f"z{first}", z[:], width)
            for t in range(PACK):
                nc.tensor.matmul_mx(
                    h_bank[t][:, first : first + width],
                    lhsT=w1_codes[:, t * P : (t + 1) * P].bitcast(FP8X4),
                    lhsT_scale=w1_plane[:, t * P : (t + 1) * P],
                    rhs=z_codes[:].bitcast(FP8X4),
                    rhs_scale=z_plane[:],
                    start=False,
                    stop=(first + width == S),
                )
        for t in range(PACK):
            nc.vector.tensor_copy(h_rows[t][:], h_bank[t][:])

        out_rows = out.rearrange("(p t) n -> p t n", t=PACK)
        for t in range(PACK):
            width = HALF if t + 1 < PACK else HALF // 2
            for begin in [0, HALF] if t + 1 < PACK else [0, HALF, HALF + HALF // 2]:
                width = HALF if (t + 1 < PACK or begin == 0) else HALF // 2
                sg = keep.tile([P, width], F32, name=f"sg{t}_{begin}")
                nc.scalar.activation(
                    sg[:],
                    h_rows[t][:].indirect(n3_t[:, begin // 16 : (begin + width) // 16]),
                    ACT.Sigmoid,
                    bias=sg_bias[:, t : t + 1],
                    scale=sl_t[:, t : t + 1],
                )
                result = keep.tile([P, width], F32, name=f"result{t}_{begin}")
                at = begin % HALF
                nc.vector.tensor_tensor(result[:], h_part(t, begin // HALF)[:, at : at + width], sg[:], ALU.mult)
                nc.sync.dma_start(out_rows[:, t, begin : begin + width], result[:])
